import numpy as np
import ml_dtypes


def mxq(x, axis, fmt="e4m3"):
    dtype, down = {"e4m3": (ml_dtypes.float8_e4m3fn, 7), "e5m2": (ml_dtypes.float8_e5m2, 14)}[fmt]
    v = np.moveaxis(np.asarray(x, np.float32).astype(ml_dtypes.bfloat16).astype(np.float64), axis, -1)
    blocks = v.reshape(v.shape[:-1] + (-1, 32))
    amax = np.abs(blocks).max(-1, keepdims=True)
    byte = np.maximum(np.where(amax > 0, np.frexp(amax)[1] - 1 + 127, 0) - down, 1)
    scale = np.exp2(byte - 127.0)
    codes = (blocks / scale).astype(np.float32).astype(dtype).astype(np.float64)
    return np.moveaxis((codes * scale).reshape(v.shape), -1, axis)


WIDE = False


def mx_kscale(k):
    if not WIDE:
        return np.ones(k)
    levels = np.array([10, -10, 5, -5, 0])
    if k % 512:
        return np.exp2(np.random.permutation(np.resize(levels, k // 32))).repeat(32)
    a = np.empty((k // 512, 16))
    for p in range(k // 512):
        a[p, :8] = np.random.permutation(np.resize(levels, 8))
        for g in range(8):
            far = levels[np.abs(levels - a[p, g]) >= 10]
            a[p, g + 8] = far[np.random.randint(len(far))]
    return np.exp2(a.ravel()).repeat(32)


def f64(x):
    return np.asarray(x).astype(np.float64)


def striped8(idx):
    return np.asarray(idx).reshape(8, -1, 16).transpose(0, 2, 1).reshape(128, -1).astype(np.uint16)


def unstriped8(offs):
    return offs.reshape(8, 16, -1).transpose(0, 2, 1).reshape(8, -1).astype(np.int64)


def pick8(x, idx, run):
    r = np.arange(len(x))
    return x[r[:, None], idx[r % (8 * run) // run]]


E2M1 = np.array([0.0, 0.5, 1.0, 1.5, 2.0, 3.0, 4.0, 6.0, -0.0, -0.5, -1.0, -1.5, -2.0, -3.0, -4.0, -6.0])


def pack_weight(w, fmt):
    k, n = w.shape
    w = f64(np.asarray(w, np.float32).astype(ml_dtypes.bfloat16)).reshape(k // 32, 32, n)
    amax = np.abs(w).max(1)
    if fmt == "e4m3":
        byte = np.frexp(amax)[1] - 1 + 127 - 7
    else:
        mant, ex = np.frexp(amax / 6.0)
        byte = np.where(mant > 0.5, ex, ex - 1) + 127
    byte = np.clip(np.where(amax > 0, byte, 1), 1, 254)
    scaled = (w * np.exp2(127.0 - byte)[:, None, :]).reshape(k, n).astype(np.float32)
    by_word = np.ascontiguousarray(scaled.reshape(k // 512, 128, 4, n).transpose(0, 1, 3, 2))
    if fmt == "e4m3":
        words = by_word.astype(ml_dtypes.float8_e4m3fn).view(np.uint8)
    else:
        c = by_word.astype(ml_dtypes.float4_e2m1fn).view(np.uint8) & 0xF
        words = (c[..., 0::2] | (c[..., 1::2] << 4)).reshape(k // 512, 128, 2 * n)
    return np.ascontiguousarray(words), np.ascontiguousarray(byte.astype(np.uint8).reshape(k // 512, 16, n))


def unpack_weight(words, scales, fmt):
    g, _, n = scales.shape
    words = np.ascontiguousarray(words).reshape(g, 128, n, -1)
    if fmt == "e4m3":
        vals = words.view(ml_dtypes.float8_e4m3fn).astype(np.float64)
    else:
        nib = np.empty((g, 128, n, 4), np.uint8)
        nib[..., 0::2] = words & 0xF
        nib[..., 1::2] = words >> 4
        vals = E2M1[nib]
    vals = vals * np.repeat(np.exp2(scales.astype(np.float64) - 127.0), 8, axis=1)[..., None]
    return vals.transpose(0, 1, 3, 2).reshape(g * 512, n)


def sigmoid(v):
    return 1.0 / (1.0 + np.exp(-v))


D, T, U, X, I, Q = 512, 1024, 1024, 1024, 512, 128


def setup_inputs():
    n = np.random.standard_normal
    idx = np.stack([np.random.permutation(T)[:I] for _ in range(8)])
    idx2 = np.stack([np.random.permutation(U)[:I] for _ in range(8)])
    idx3 = np.stack([np.random.permutation(X)[:I] for _ in range(8)])
    idx4 = np.stack([np.random.permutation(U)[:I] for _ in range(8)])
    idx5 = np.stack([np.random.permutation(T)[:I] for _ in range(8)])
    fd = mx_kscale(D)
    keysp = pack_weight(n((D, T)) / fd[:, None], "e2m1")
    notesp = pack_weight(n((D, U)) / fd[:, None], "e4m3")
    usersp = pack_weight(n((D, X)) / fd[:, None], "e2m1")
    return {
        "query": (n((D, Q)) * 1.0 / np.sqrt(D) * fd[:, None]).astype(np.float32),
        "keys_words": keysp[0],
        "keys_scales": keysp[1],
        "notes_words": notesp[0],
        "notes_scales": notesp[1],
        "users_words": usersp[0],
        "users_scales": usersp[1],
        "thr": (np.random.uniform(-0.6, 0.6, (Q, 1))).astype(np.float32),
        "slope": (np.random.uniform(1.0, 3.0, (Q, 1))).astype(np.float32),
        "offs": striped8(idx),
        "offs2": striped8(idx2),
        "offs3": striped8(idx3),
        "offs4": striped8(idx4),
        "offs5": striped8(idx5),
    }


def reference(query, keys_words, keys_scales, notes_words, notes_scales, users_words, users_scales, thr, slope, offs, offs2, offs3, offs4, offs5):
    idx = unstriped8(offs)
    idx2 = unstriped8(offs2)
    idx3 = unstriped8(offs3)
    idx4 = unstriped8(offs4)
    idx5 = unstriped8(offs5)
    keysu = unpack_weight(keys_words, keys_scales, "e2m1")
    notesu = unpack_weight(notes_words, notes_scales, "e4m3")
    usersu = unpack_weight(users_words, users_scales, "e2m1")
    queryq = mxq(f64(query), 0, "e4m3")
    a = queryq.T @ keysu
    b = queryq.T @ notesu
    c0 = queryq.T @ usersu
    s1 = sigmoid(pick8(c0, idx3, 16) * f64(slope) + f64(thr))
    r = pick8(a, idx, 16) - pick8(b, idx2, 16)
    w = r * s1
    f1 = np.zeros((Q, U))
    f1[np.arange(Q)[:, None], idx2[np.arange(Q) % 128 // 16]] = w
    bb = b + f1
    y = pick8(bb, idx4, 16) - pick8(a, idx5, 16)
    return y

@@ -1,0 +1,138 @@
+from contextlib import ExitStack
+
+import concourse.mybir as mybir
+
+D, T, I, Q = 512, 1024, 512, 128
+FLOPS = 2 * D * Q * 3 * T
+
+F32 = mybir.dt.float32
+BF16 = mybir.dt.bfloat16
+I32 = mybir.dt.int32
+U32 = mybir.dt.uint32
+U16 = mybir.dt.uint16
+U8 = mybir.dt.uint8
+FP8X4 = mybir.dt.float8_e4m3fn_x4
+FP4X4 = mybir.dt.float4_e2m1fn_x4
+ALU = mybir.AluOpType
+ACT = mybir.ActivationFunctionType
+
+P = 128
+HALF = I // 2
+HCOLS = HALF // 16
+
+
+def tile_attend_blendgate_three_kernel(tc, query, keys_words, keys_scales, notes_words, notes_scales,
+                                        users_words, users_scales, thr, slope, offs, offs2, offs3, offs4, offs5, out):
+    nc = tc.nc
+    with ExitStack() as ctx:
+        sb = ctx.enter_context(tc.tile_pool(name="sb", bufs=1))
+        ps = ctx.enter_context(tc.psum_pool(name="ps", bufs=1))
+
+        planes = {}
+        for name in ("notes", "keys", "users"):
+            planes[name] = sb.tile([P, T], U8, name=name + "_plane", align_bytes=64)
+            nc.vector.memset(planes[name][:].bitcast(I32), 0)
+
+        def load_plane(name, scales):
+            rows = scales[0].bitcast(I32)
+            for quad in range(4):
+                nc.sync.dma_start(planes[name][32 * quad:32 * quad + 4, :].bitcast(I32), rows[4 * quad:4 * quad + 4, :])
+
+        q_raw = sb.tile([P, 4, Q], F32)
+        nc.sync.dma_start(q_raw[:], query.rearrange("(p j) q -> p j q", j=4))
+
+        notes_flat = notes_words[0].rearrange("p n t -> p (n t)")
+        notes_w = []
+        for h in range(2):
+            w = sb.tile([P, 4 * 512], U8, name="notes_w%d" % h, align_bytes=64)
+            notes_w.append(w)
+        nc.sync.dma_start(notes_w[0][:].bitcast(I32), notes_flat[:, 0:2048].bitcast(I32))
+        load_plane("notes", notes_scales)
+        nc.sync.dma_start(notes_w[1][:].bitcast(I32), notes_flat[:, 2048:4096].bitcast(I32))
+        keys_w = sb.tile([P, 2 * T], U8, align_bytes=64)
+        load_plane("keys", keys_scales)
+        nc.gpsimd.dma_start(keys_w[:].bitcast(I32), keys_words[0].bitcast(I32))
+        users_w = sb.tile([P, 2 * T], U8, align_bytes=64)
+        load_plane("users", users_scales)
+        nc.gpsimd.dma_start(users_w[:].bitcast(I32), users_words[0].bitcast(I32))
+
+        f1 = sb.tile([P, T], F32)
+        nc.gpsimd.memset(f1[:], 0.0)
+
+        lists = {}
+        thr_t = sb.tile([P, 1], F32)
+        slope_t = sb.tile([P, 1], F32)
+        for name, src in (("l2", offs2), ("l1", offs), ("l3", offs3), ("l5", offs5), ("l4", offs4)):
+            lists[name] = sb.tile([P, I // 16], U16, name=name)
+            nc.sync.dma_start(lists[name][:], src)
+            if name == "l3":
+                nc.sync.dma_start(thr_t[:], thr)
+                nc.sync.dma_start(slope_t[:], slope)
+
+        q_bf = sb.tile([P, Q, 4], BF16, align_bytes=64)
+        nc.vector.tensor_copy(q_bf[:], q_raw[:].rearrange("p j q -> p q j"))
+        q_codes = sb.tile([P, Q], U32, align_bytes=64)
+        q_plane = sb.tile([P, Q], U8, align_bytes=64)
+        nc.vector.quantize_mx(out=q_codes[:].bitcast(FP8X4), scales=q_plane[:],
+                              in_=q_bf[:].rearrange("p q j -> p (q j)"))
+
+        def score(bank, words, plane):
+            nc.tensor.matmul_mx(out=bank, lhsT=q_codes[:].bitcast(FP8X4), lhsT_scale=q_plane[:],
+                                rhs=words, rhs_scale=plane, start=True, stop=True)
+
+        a = sb.tile([P, T], F32)
+        b = sb.tile([P, T], F32)
+        c0 = sb.tile([P, T], F32, tag="c0_then_ga5")
+        b_ps = []
+        for h in range(2):
+            bank = ps.tile([P, 512], F32, name="b_ps%d" % h)
+            b_ps.append(bank)
+            score(bank[:], notes_w[h][:].bitcast(FP8X4), planes["notes"][:, 512 * h:512 * h + 512])
+        nc.scalar.copy(b[:, 0:512], b_ps[0][:])
+        nc.vector.tensor_copy(b[:, 512:1024], b_ps[1][:])
+
+        def half(name, h):
+            return lists[name][:, HCOLS * h:HCOLS * (h + 1)]
+
+        gb = sb.tile([P, I], F32)
+        for h in range(2):
+            nc.scalar.activation(gb[:, HALF * h:HALF * (h + 1)], b[:].indirect(half("l2", h)), ACT.Copy)
+
+        for h in range(2):
+            bank = ps.tile([P, 512], F32, name="a_ps%d" % h)
+            score(bank[:], keys_w[:, 1024 * h:1024 * h + 1024].bitcast(FP4X4), planes["keys"][:, 512 * h:512 * h + 512])
+            nc.vector.tensor_copy(a[:, 512 * h:512 * h + 512], bank[:])
+
+        r = sb.tile([P, I], F32)
+        nc.vector.tensor_tensor(r[:, 0:HALF], a[:].indirect(half("l1", 0)), gb[:, 0:HALF], ALU.subtract)
+
+        for u in range(4):
+            bank = ps.tile([P, 256], F32, name="c_ps%d" % u)
+            score(bank[:], users_w[:, 512 * u:512 * u + 512].bitcast(FP4X4), planes["users"][:, 256 * u:256 * u + 256])
+            if u == 2:
+                nc.vector.tensor_copy(c0[:, 256 * u:256 * u + 256], bank[:])
+            else:
+                nc.scalar.copy(c0[:, 256 * u:256 * u + 256], bank[:])
+
+        nc.vector.tensor_tensor(r[:, HALF:I], a[:].indirect(half("l1", 1)), gb[:, HALF:I], ALU.subtract)
+
+        s1 = sb.tile([P, I], F32)
+        for h in range(2):
+            cols = slice(HALF * h, HALF * (h + 1))
+            nc.scalar.activation(s1[:, cols], c0[:].indirect(half("l3", h)), ACT.Sigmoid, bias=thr_t[:], scale=slope_t[:])
+            nc.vector.tensor_tensor(f1[:].indirect(half("l2", h)), r[:, cols], s1[:, cols], ALU.mult)
+
+        ga5 = sb.tile([P, I], F32, tag="c0_then_ga5")
+        nc.scalar.activation(ga5[:], a[:].indirect(lists["l5"][:]), ACT.Copy)
+
+        bb = sb.tile([P, T], F32)
+        nc.vector.tensor_tensor(bb[:], b[:], f1[:], ALU.add)
+
+        y0 = sb.tile([P, HALF], F32)
+        y1 = sb.tile([P, HALF], F32)
+        g4 = sb.tile([P, HALF], F32)
+        nc.vector.tensor_tensor(y0[:], bb[:].indirect(half("l4", 0)), ga5[:, 0:HALF], ALU.subtract)
+        nc.sync.dma_start(out[:, 0:HALF], y0[:])
+        nc.scalar.activation(g4[:], bb[:].indirect(half("l4", 1)), ACT.Copy)
+        nc.vector.tensor_tensor(y1[:], g4[:], ga5[:, HALF:I], ALU.subtract)
+        nc.sync.dma_start(out[:, HALF:I], y1[:])

@@ -41,33 +41,35 @@ def tile_attend_blendgate_three_kernel(tc, query, keys_words, keys_scales, notes
         q_raw = sb.tile([P, 4, Q], F32)
         nc.sync.dma_start(q_raw[:], query.rearrange("(p j) q -> p j q", j=4))
 
-        notes_flat = notes_words[0].rearrange("p n t -> p (n t)")
-        notes_w = []
-        for h in range(2):
-            w = sb.tile([P, 4 * 512], U8, name="notes_w%d" % h, align_bytes=64)
-            notes_w.append(w)
-        nc.sync.dma_start(notes_w[0][:].bitcast(I32), notes_flat[:, 0:2048].bitcast(I32))
-        load_plane("notes", notes_scales)
-        nc.sync.dma_start(notes_w[1][:].bitcast(I32), notes_flat[:, 2048:4096].bitcast(I32))
-        keys_w = sb.tile([P, 2 * T], U8, align_bytes=64)
-        load_plane("keys", keys_scales)
-        nc.gpsimd.dma_start(keys_w[:].bitcast(I32), keys_words[0].bitcast(I32))
-        users_w = sb.tile([P, 2 * T], U8, align_bytes=64)
-        load_plane("users", users_scales)
-        nc.gpsimd.dma_start(users_w[:].bitcast(I32), users_words[0].bitcast(I32))
-
-        f1 = sb.tile([P, T], F32)
-        nc.gpsimd.memset(f1[:], 0.0)
-
         lists = {}
-        thr_t = sb.tile([P, 1], F32)
-        slope_t = sb.tile([P, 1], F32)
-        for name, src in (("l2", offs2), ("l1", offs), ("l3", offs3), ("l5", offs5), ("l4", offs4)):
+
+        def load_list(name, src):
             lists[name] = sb.tile([P, I // 16], U16, name=name)
             nc.sync.dma_start(lists[name][:], src)
-            if name == "l3":
-                nc.sync.dma_start(thr_t[:], thr)
-                nc.sync.dma_start(slope_t[:], slope)
+
+        notes_lo = sb.tile([P, 2 * T], U8, align_bytes=64)
+        notes_hi = sb.tile([P, 2 * T], U8, align_bytes=64)
+        notes_flat = notes_words[0].rearrange("p n t -> p (n t)")
+        keys_w = sb.tile([P, 2 * T], U8, align_bytes=64)
+        users_w = sb.tile([P, 2 * T], U8, align_bytes=64)
+        thr_t = sb.tile([P, 1], F32)
+        slope_t = sb.tile([P, 1], F32)
+        f1 = sb.tile([P, T], F32)
+        nc.sync.dma_start(notes_lo[:].bitcast(I32), notes_flat[:, 0:2 * T].bitcast(I32))
+        nc.gpsimd.dma_start(keys_w[:].bitcast(I32), keys_words[0].bitcast(I32))
+        nc.gpsimd.dma_start(users_w[:].bitcast(I32), users_words[0].bitcast(I32))
+        nc.gpsimd.memset(f1[:], 0.0)
+        load_plane("notes", notes_scales)
+        nc.sync.dma_start(notes_hi[:].bitcast(I32), notes_flat[:, 2 * T:4 * T].bitcast(I32))
+        load_list("l2", offs2)
+        load_plane("keys", keys_scales)
+        load_list("l1", offs)
+        load_plane("users", users_scales)
+        load_list("l3", offs3)
+        nc.sync.dma_start(thr_t[:], thr)
+        nc.sync.dma_start(slope_t[:], slope)
+        load_list("l5", offs5)
+        load_list("l4", offs4)
 
         q_bf = sb.tile([P, Q, 4], BF16, align_bytes=64)
         nc.vector.tensor_copy(q_bf[:], q_raw[:].rearrange("p j q -> p q j"))
@@ -80,41 +82,37 @@ def tile_attend_blendgate_three_kernel(tc, query, keys_words, keys_scales, notes
             nc.tensor.matmul_mx(out=bank, lhsT=q_codes[:].bitcast(FP8X4), lhsT_scale=q_plane[:],
                                 rhs=words, rhs_scale=plane, start=True, stop=True)
 
-        a = sb.tile([P, T], F32)
-        b = sb.tile([P, T], F32)
-        c0 = sb.tile([P, T], F32, tag="c0_then_ga5")
-        b_ps = []
-        for h in range(2):
-            bank = ps.tile([P, 512], F32, name="b_ps%d" % h)
-            b_ps.append(bank)
-            score(bank[:], notes_w[h][:].bitcast(FP8X4), planes["notes"][:, 512 * h:512 * h + 512])
-        nc.scalar.copy(b[:, 0:512], b_ps[0][:])
-        nc.vector.tensor_copy(b[:, 512:1024], b_ps[1][:])
+        warm = sb.tile([P, 1], F32)
+        nc.scalar.activation(warm[:], q_raw[:, 0, 0:1], ACT.Sigmoid)
+
+        def scores(dst, name, c, width, words, copy):
+            bank = ps.tile([P, width], F32, name="%s_bank%d" % (name, c))
+            score(bank[:], words, planes[name][:, c:c + width])
+            copy(dst[:, c:c + width], bank[:])
+            return bank
 
         def half(name, h):
             return lists[name][:, HCOLS * h:HCOLS * (h + 1)]
 
+        on_v, on_s = nc.vector.tensor_copy, nc.scalar.copy
+        b = sb.tile([P, T], F32, tag="b_c0_ga5")
+        b_banks = [
+            (0, 512, scores(b, "notes", 0, 512, notes_lo[:].bitcast(FP8X4), on_s)),
+            (512, 256, scores(b, "notes", 512, 256, notes_hi[:, 0:T].bitcast(FP8X4), on_v)),
+            (768, 256, scores(b, "notes", 768, 256, notes_hi[:, T:2 * T].bitcast(FP8X4), on_v)),
+        ]
         gb = sb.tile([P, I], F32)
-        for h in range(2):
-            nc.scalar.activation(gb[:, HALF * h:HALF * (h + 1)], b[:].indirect(half("l2", h)), ACT.Copy)
+        nc.scalar.activation(gb[:], b[:].indirect(lists["l2"][:]), ACT.Copy)
 
+        a = sb.tile([P, T], F32)
         for h in range(2):
-            bank = ps.tile([P, 512], F32, name="a_ps%d" % h)
-            score(bank[:], keys_w[:, 1024 * h:1024 * h + 1024].bitcast(FP4X4), planes["keys"][:, 512 * h:512 * h + 512])
-            nc.vector.tensor_copy(a[:, 512 * h:512 * h + 512], bank[:])
+            scores(a, "keys", 512 * h, 512, keys_w[:, 1024 * h:1024 * h + 1024].bitcast(FP4X4), on_v)
+        c0 = sb.tile([P, T], F32, tag="b_c0_ga5")
+        for h in range(2):
+            scores(c0, "users", 512 * h, 512, users_w[:, 1024 * h:1024 * h + 1024].bitcast(FP4X4), on_s)
 
         r = sb.tile([P, I], F32)
-        nc.vector.tensor_tensor(r[:, 0:HALF], a[:].indirect(half("l1", 0)), gb[:, 0:HALF], ALU.subtract)
-
-        for u in range(4):
-            bank = ps.tile([P, 256], F32, name="c_ps%d" % u)
-            score(bank[:], users_w[:, 512 * u:512 * u + 512].bitcast(FP4X4), planes["users"][:, 256 * u:256 * u + 256])
-            if u == 2:
-                nc.vector.tensor_copy(c0[:, 256 * u:256 * u + 256], bank[:])
-            else:
-                nc.scalar.copy(c0[:, 256 * u:256 * u + 256], bank[:])
-
-        nc.vector.tensor_tensor(r[:, HALF:I], a[:].indirect(half("l1", 1)), gb[:, HALF:I], ALU.subtract)
+        nc.vector.tensor_tensor(r[:], a[:].indirect(lists["l1"][:]), gb[:], ALU.subtract)
 
         s1 = sb.tile([P, I], F32)
         for h in range(2):
@@ -122,11 +120,12 @@ def tile_attend_blendgate_three_kernel(tc, query, keys_words, keys_scales, notes
             nc.scalar.activation(s1[:, cols], c0[:].indirect(half("l3", h)), ACT.Sigmoid, bias=thr_t[:], scale=slope_t[:])
             nc.vector.tensor_tensor(f1[:].indirect(half("l2", h)), r[:, cols], s1[:, cols], ALU.mult)
 
-        ga5 = sb.tile([P, I], F32, tag="c0_then_ga5")
+        ga5 = sb.tile([P, I], F32, tag="b_c0_ga5")
         nc.scalar.activation(ga5[:], a[:].indirect(lists["l5"][:]), ACT.Copy)
 
         bb = sb.tile([P, T], F32)
-        nc.vector.tensor_tensor(bb[:], b[:], f1[:], ALU.add)
+        for c, width, bank in b_banks:
+            nc.vector.tensor_tensor(bb[:, c:c + width], bank[:], f1[:, c:c + width], ALU.add)
 
         y0 = sb.tile([P, HALF], F32)
         y1 = sb.tile([P, HALF], F32)

@@ -33,9 +33,9 @@ def tile_attend_blendgate_three_kernel(tc, query, keys_words, keys_scales, notes
             planes[name] = sb.tile([P, T], U8, name=name + "_plane", align_bytes=64)
             nc.vector.memset(planes[name][:].bitcast(I32), 0)
 
-        def load_plane(name, scales):
+        def load_plane(name, scales, quads=range(4)):
             rows = scales[0].bitcast(I32)
-            for quad in range(4):
+            for quad in quads:
                 nc.sync.dma_start(planes[name][32 * quad:32 * quad + 4, :].bitcast(I32), rows[4 * quad:4 * quad + 4, :])
 
         q_raw = sb.tile([P, 4, Q], F32)
@@ -55,24 +55,29 @@ def tile_attend_blendgate_three_kernel(tc, query, keys_words, keys_scales, notes
         thr_t = sb.tile([P, 1], F32)
         slope_t = sb.tile([P, 1], F32)
         f1 = sb.tile([P, T], F32)
-        nc.sync.dma_start(notes_lo[:].bitcast(I32), notes_flat[:, 0:2 * T].bitcast(I32))
         nc.gpsimd.dma_start(keys_w[:].bitcast(I32), keys_words[0].bitcast(I32))
         nc.gpsimd.dma_start(users_w[:].bitcast(I32), users_words[0].bitcast(I32))
-        nc.gpsimd.memset(f1[:], 0.0)
-        load_plane("notes", notes_scales)
-        nc.sync.dma_start(notes_hi[:].bitcast(I32), notes_flat[:, 2 * T:4 * T].bitcast(I32))
+        nc.gpsimd.dma_start(thr_t[:], thr)
+        nc.gpsimd.dma_start(slope_t[:], slope)
+        nc.vector.memset(f1[:], 0.0)
+        load_plane("notes", notes_scales, range(3))
+        nc.sync.dma_start(notes_lo[:].bitcast(I32), notes_flat[:, 0:2 * T].bitcast(I32))
+        load_plane("notes", notes_scales, range(3, 4))
         load_list("l2", offs2)
+        nc.sync.dma_start(notes_hi[:].bitcast(I32), notes_flat[:, 2 * T:4 * T].bitcast(I32))
         load_plane("keys", keys_scales)
-        load_list("l1", offs)
         load_plane("users", users_scales)
+        load_list("l1", offs)
         load_list("l3", offs3)
-        nc.sync.dma_start(thr_t[:], thr)
-        nc.sync.dma_start(slope_t[:], slope)
         load_list("l5", offs5)
         load_list("l4", offs4)
 
         q_bf = sb.tile([P, Q, 4], BF16, align_bytes=64)
-        nc.vector.tensor_copy(q_bf[:], q_raw[:].rearrange("p j q -> p q j"))
+        warm = sb.tile([P, 1], F32)
+        nc.scalar.activation(warm[:], q_raw[:, 0, 0:1], ACT.Sigmoid)
+        q_woven = q_raw[:].rearrange("p j q -> p q j")
+        nc.vector.tensor_copy(q_bf[:, 0:80, :], q_woven[:, 0:80, :])
+        nc.scalar.copy(q_bf[:, 80:Q, :], q_woven[:, 80:Q, :])
         q_codes = sb.tile([P, Q], U32, align_bytes=64)
         q_plane = sb.tile([P, Q], U8, align_bytes=64)
         nc.vector.quantize_mx(out=q_codes[:].bitcast(FP8X4), scales=q_plane[:],
@@ -81,9 +86,6 @@ def tile_attend_blendgate_three_kernel(tc, query, keys_words, keys_scales, notes
         def score(bank, words, plane):
             nc.tensor.matmul_mx(out=bank, lhsT=q_codes[:].bitcast(FP8X4), lhsT_scale=q_plane[:],
                                 rhs=words, rhs_scale=plane, start=True, stop=True)
-
-        warm = sb.tile([P, 1], F32)
-        nc.scalar.activation(warm[:], q_raw[:, 0, 0:1], ACT.Sigmoid)
 
         def scores(dst, name, c, width, words, copy):
             bank = ps.tile([P, width], F32, name="%s_bank%d" % (name, c))
@@ -112,7 +114,9 @@ def tile_attend_blendgate_three_kernel(tc, query, keys_words, keys_scales, notes
             scores(c0, "users", 512 * h, 512, users_w[:, 1024 * h:1024 * h + 1024].bitcast(FP4X4), on_s)
 
         r = sb.tile([P, I], F32)
-        nc.vector.tensor_tensor(r[:], a[:].indirect(lists["l1"][:]), gb[:], ALU.subtract)
+        for h in range(2):
+            cols = slice(HALF * h, HALF * (h + 1))
+            nc.vector.tensor_tensor(r[:, cols], a[:].indirect(half("l1", h)), gb[:, cols], ALU.subtract)
 
         s1 = sb.tile([P, I], F32)
         for h in range(2):
@@ -120,18 +124,23 @@ def tile_attend_blendgate_three_kernel(tc, query, keys_words, keys_scales, notes
             nc.scalar.activation(s1[:, cols], c0[:].indirect(half("l3", h)), ACT.Sigmoid, bias=thr_t[:], scale=slope_t[:])
             nc.vector.tensor_tensor(f1[:].indirect(half("l2", h)), r[:, cols], s1[:, cols], ALU.mult)
 
-        ga5 = sb.tile([P, I], F32, tag="b_c0_ga5")
-        nc.scalar.activation(ga5[:], a[:].indirect(lists["l5"][:]), ACT.Copy)
+        late = sb.tile([P, I + 256], F32, tag="b_c0_ga5")
+        ga5 = late[:, 0:I]
+        nc.scalar.activation(ga5, a[:].indirect(lists["l5"][:]), ACT.Copy)
 
         bb = sb.tile([P, T], F32)
-        for c, width, bank in b_banks:
+        c, width, bank = b_banks[2]
+        b_tail = late[:, I:I + width]
+        nc.scalar.copy(b_tail, bank[:])
+        nc.gpsimd.tensor_tensor(bb[:, c:c + width], b_tail, f1[:, c:c + width], ALU.add)
+        for c, width, bank in b_banks[0:2]:
             nc.vector.tensor_tensor(bb[:, c:c + width], bank[:], f1[:, c:c + width], ALU.add)
 
         y0 = sb.tile([P, HALF], F32)
         y1 = sb.tile([P, HALF], F32)
         g4 = sb.tile([P, HALF], F32)
-        nc.vector.tensor_tensor(y0[:], bb[:].indirect(half("l4", 0)), ga5[:, 0:HALF], ALU.subtract)
+        nc.vector.tensor_tensor(y0[:], bb[:].indirect(half("l4", 0)), late[:, 0:HALF], ALU.subtract)
         nc.sync.dma_start(out[:, 0:HALF], y0[:])
         nc.scalar.activation(g4[:], bb[:].indirect(half("l4", 1)), ACT.Copy)
-        nc.vector.tensor_tensor(y1[:], g4[:], ga5[:, HALF:I], ALU.subtract)
+        nc.vector.tensor_tensor(y1[:], g4[:], late[:, HALF:I], ALU.subtract)
         nc.sync.dma_start(out[:, HALF:I], y1[:])

@@ -2,8 +2,8 @@ from contextlib import ExitStack
 
 import concourse.mybir as mybir
 
-D, T, I, Q = 512, 1024, 512, 128
-FLOPS = 2 * D * Q * 3 * T
+D, POOL, SLOTS, ROWS = 512, 1024, 512, 128
+FLOPS = 2 * D * ROWS * 3 * POOL
 
 F32 = mybir.dt.float32
 BF16 = mybir.dt.bfloat16
@@ -17,8 +17,12 @@ ALU = mybir.AluOpType
 ACT = mybir.ActivationFunctionType
 
 P = 128
-HALF = I // 2
-HCOLS = HALF // 16
+PACK = 4
+BANK = 512
+QUARTER = POOL // 4
+HALF = SLOTS // 2
+HALF_COLS = HALF // 16
+CAST_ON_VECTOR = 80
 
 
 def tile_attend_blendgate_three_kernel(tc, query, keys_words, keys_scales, notes_words, notes_scales,
@@ -30,117 +34,110 @@ def tile_attend_blendgate_three_kernel(tc, query, keys_words, keys_scales, notes
 
         planes = {}
         for name in ("notes", "keys", "users"):
-            planes[name] = sb.tile([P, T], U8, name=name + "_plane", align_bytes=64)
+            planes[name] = sb.tile([P, POOL], U8, name=name + "_plane", align_bytes=64)
             nc.vector.memset(planes[name][:].bitcast(I32), 0)
 
-        def load_plane(name, scales, quads=range(4)):
+        def load_plane(name, scales, quadrants):
             rows = scales[0].bitcast(I32)
-            for quad in quads:
+            for quad in quadrants:
                 nc.sync.dma_start(planes[name][32 * quad:32 * quad + 4, :].bitcast(I32), rows[4 * quad:4 * quad + 4, :])
-
-        q_raw = sb.tile([P, 4, Q], F32)
-        nc.sync.dma_start(q_raw[:], query.rearrange("(p j) q -> p j q", j=4))
 
         lists = {}
 
         def load_list(name, src):
-            lists[name] = sb.tile([P, I // 16], U16, name=name)
+            lists[name] = sb.tile([P, SLOTS // 16], U16, name=name)
             nc.sync.dma_start(lists[name][:], src)
 
-        notes_lo = sb.tile([P, 2 * T], U8, align_bytes=64)
-        notes_hi = sb.tile([P, 2 * T], U8, align_bytes=64)
+        def half_list(name, h):
+            return lists[name][:, HALF_COLS * h:HALF_COLS * (h + 1)]
+
+        q_raw = sb.tile([P, PACK, ROWS], F32)
+        nc.sync.dma_start(q_raw[:], query.rearrange("(p j) q -> p j q", j=PACK))
+
+        notes_lo = sb.tile([P, PACK * BANK], U8, align_bytes=64)
+        notes_hi = sb.tile([P, PACK * BANK], U8, align_bytes=64)
         notes_flat = notes_words[0].rearrange("p n t -> p (n t)")
-        keys_w = sb.tile([P, 2 * T], U8, align_bytes=64)
-        users_w = sb.tile([P, 2 * T], U8, align_bytes=64)
+        keys_w = sb.tile([P, 2 * POOL], U8, align_bytes=64)
+        users_w = sb.tile([P, 2 * POOL], U8, align_bytes=64)
         thr_t = sb.tile([P, 1], F32)
         slope_t = sb.tile([P, 1], F32)
-        f1 = sb.tile([P, T], F32)
+        f1 = sb.tile([P, POOL], F32)
         nc.gpsimd.dma_start(keys_w[:].bitcast(I32), keys_words[0].bitcast(I32))
         nc.gpsimd.dma_start(users_w[:].bitcast(I32), users_words[0].bitcast(I32))
         nc.gpsimd.dma_start(thr_t[:], thr)
         nc.gpsimd.dma_start(slope_t[:], slope)
         nc.vector.memset(f1[:], 0.0)
         load_plane("notes", notes_scales, range(3))
-        nc.sync.dma_start(notes_lo[:].bitcast(I32), notes_flat[:, 0:2 * T].bitcast(I32))
+        nc.sync.dma_start(notes_lo[:].bitcast(I32), notes_flat[:, 0:PACK * BANK].bitcast(I32))
         load_plane("notes", notes_scales, range(3, 4))
-        load_list("l2", offs2)
-        nc.sync.dma_start(notes_hi[:].bitcast(I32), notes_flat[:, 2 * T:4 * T].bitcast(I32))
-        load_plane("keys", keys_scales)
-        load_plane("users", users_scales)
-        load_list("l1", offs)
-        load_list("l3", offs3)
-        load_list("l5", offs5)
-        load_list("l4", offs4)
+        load_list("idx2", offs2)
+        nc.sync.dma_start(notes_hi[:].bitcast(I32), notes_flat[:, PACK * BANK:PACK * POOL].bitcast(I32))
+        load_plane("keys", keys_scales, range(4))
+        load_plane("users", users_scales, range(4))
+        load_list("idx", offs)
+        load_list("idx3", offs3)
+        load_list("idx5", offs5)
+        load_list("idx4", offs4)
 
-        q_bf = sb.tile([P, Q, 4], BF16, align_bytes=64)
+        q_bf = sb.tile([P, ROWS, PACK], BF16, align_bytes=64)
         warm = sb.tile([P, 1], F32)
         nc.scalar.activation(warm[:], q_raw[:, 0, 0:1], ACT.Sigmoid)
         q_woven = q_raw[:].rearrange("p j q -> p q j")
-        nc.vector.tensor_copy(q_bf[:, 0:80, :], q_woven[:, 0:80, :])
-        nc.scalar.copy(q_bf[:, 80:Q, :], q_woven[:, 80:Q, :])
-        q_codes = sb.tile([P, Q], U32, align_bytes=64)
-        q_plane = sb.tile([P, Q], U8, align_bytes=64)
+        nc.vector.tensor_copy(q_bf[:, 0:CAST_ON_VECTOR, :], q_woven[:, 0:CAST_ON_VECTOR, :])
+        nc.scalar.copy(q_bf[:, CAST_ON_VECTOR:ROWS, :], q_woven[:, CAST_ON_VECTOR:ROWS, :])
+        q_codes = sb.tile([P, ROWS], U32, align_bytes=64)
+        q_plane = sb.tile([P, ROWS], U8, align_bytes=64)
         nc.vector.quantize_mx(out=q_codes[:].bitcast(FP8X4), scales=q_plane[:],
                               in_=q_bf[:].rearrange("p q j -> p (q j)"))
 
-        def score(bank, words, plane):
-            nc.tensor.matmul_mx(out=bank, lhsT=q_codes[:].bitcast(FP8X4), lhsT_scale=q_plane[:],
-                                rhs=words, rhs_scale=plane, start=True, stop=True)
-
-        def scores(dst, name, c, width, words, copy):
-            bank = ps.tile([P, width], F32, name="%s_bank%d" % (name, c))
-            score(bank[:], words, planes[name][:, c:c + width])
-            copy(dst[:, c:c + width], bank[:])
+        def scores(dst, name, first, width, words, copy):
+            bank = ps.tile([P, width], F32, name="%s_bank%d" % (name, first))
+            nc.tensor.matmul_mx(out=bank[:], lhsT=q_codes[:].bitcast(FP8X4), lhsT_scale=q_plane[:],
+                                rhs=words, rhs_scale=planes[name][:, first:first + width], start=True, stop=True)
+            copy(dst[:, first:first + width], bank[:])
             return bank
 
-        def half(name, h):
-            return lists[name][:, HCOLS * h:HCOLS * (h + 1)]
+        on_vector, on_scalar = nc.vector.tensor_copy, nc.scalar.copy
 
-        on_v, on_s = nc.vector.tensor_copy, nc.scalar.copy
-        b = sb.tile([P, T], F32, tag="b_c0_ga5")
-        b_banks = [
-            (0, 512, scores(b, "notes", 0, 512, notes_lo[:].bitcast(FP8X4), on_s)),
-            (512, 256, scores(b, "notes", 512, 256, notes_hi[:, 0:T].bitcast(FP8X4), on_v)),
-            (768, 256, scores(b, "notes", 768, 256, notes_hi[:, T:2 * T].bitcast(FP8X4), on_v)),
-        ]
-        gb = sb.tile([P, I], F32)
-        nc.scalar.activation(gb[:], b[:].indirect(lists["l2"][:]), ACT.Copy)
+        b = sb.tile([P, POOL], F32)
+        b_bank_lo = scores(b, "notes", 0, BANK, notes_lo[:].bitcast(FP8X4), on_scalar)
+        b_bank_mid = scores(b, "notes", BANK, QUARTER, notes_hi[:, 0:PACK * QUARTER].bitcast(FP8X4), on_vector)
+        scores(b, "notes", BANK + QUARTER, QUARTER, notes_hi[:, PACK * QUARTER:PACK * BANK].bitcast(FP8X4), on_vector)
+        b_listed = sb.tile([P, SLOTS], F32)
+        nc.scalar.activation(b_listed[:], b[:].indirect(lists["idx2"][:]), ACT.Copy)
 
-        a = sb.tile([P, T], F32)
-        for h in range(2):
-            scores(a, "keys", 512 * h, 512, keys_w[:, 1024 * h:1024 * h + 1024].bitcast(FP4X4), on_v)
-        c0 = sb.tile([P, T], F32, tag="b_c0_ga5")
-        for h in range(2):
-            scores(c0, "users", 512 * h, 512, users_w[:, 1024 * h:1024 * h + 1024].bitcast(FP4X4), on_s)
+        a = sb.tile([P, POOL], F32)
+        for first in (0, BANK):
+            scores(a, "keys", first, BANK, keys_w[:, 2 * first:2 * (first + BANK)].bitcast(FP4X4), on_vector)
+        c0 = sb.tile([P, POOL], F32, tag="c0_then_a_last")
+        for first, width, copy in ((0, QUARTER, on_vector), (QUARTER, QUARTER, on_scalar), (BANK, BANK, on_scalar)):
+            scores(c0, "users", first, width, users_w[:, 2 * first:2 * (first + width)].bitcast(FP4X4), copy)
 
-        r = sb.tile([P, I], F32)
-        for h in range(2):
-            cols = slice(HALF * h, HALF * (h + 1))
-            nc.vector.tensor_tensor(r[:, cols], a[:].indirect(half("l1", h)), gb[:, cols], ALU.subtract)
+        halves = [slice(0, HALF), slice(HALF, SLOTS)]
+        r = sb.tile([P, SLOTS], F32)
+        for h, cols in enumerate(halves):
+            nc.vector.tensor_tensor(r[:, cols], a[:].indirect(half_list("idx", h)), b_listed[:, cols], ALU.subtract)
 
-        s1 = sb.tile([P, I], F32)
-        for h in range(2):
-            cols = slice(HALF * h, HALF * (h + 1))
-            nc.scalar.activation(s1[:, cols], c0[:].indirect(half("l3", h)), ACT.Sigmoid, bias=thr_t[:], scale=slope_t[:])
-            nc.vector.tensor_tensor(f1[:].indirect(half("l2", h)), r[:, cols], s1[:, cols], ALU.mult)
+        s1 = sb.tile([P, SLOTS], F32)
+        for h, cols in enumerate(halves):
+            nc.scalar.activation(s1[:, cols], c0[:].indirect(half_list("idx3", h)), ACT.Sigmoid,
+                                 bias=thr_t[:], scale=slope_t[:])
+            nc.vector.tensor_tensor(f1[:].indirect(half_list("idx2", h)), r[:, cols], s1[:, cols], ALU.mult)
 
-        late = sb.tile([P, I + 256], F32, tag="b_c0_ga5")
-        ga5 = late[:, 0:I]
-        nc.scalar.activation(ga5, a[:].indirect(lists["l5"][:]), ACT.Copy)
+        a_last = sb.tile([P, SLOTS], F32, tag="c0_then_a_last")
+        nc.scalar.activation(a_last[:], a[:].indirect(lists["idx5"][:]), ACT.Copy)
 
-        bb = sb.tile([P, T], F32)
-        c, width, bank = b_banks[2]
-        b_tail = late[:, I:I + width]
-        nc.scalar.copy(b_tail, bank[:])
-        nc.gpsimd.tensor_tensor(bb[:, c:c + width], b_tail, f1[:, c:c + width], ALU.add)
-        for c, width, bank in b_banks[0:2]:
-            nc.vector.tensor_tensor(bb[:, c:c + width], bank[:], f1[:, c:c + width], ALU.add)
+        bb = sb.tile([P, POOL], F32)
+        tail = slice(BANK + QUARTER, POOL)
+        nc.gpsimd.tensor_tensor(bb[:, tail], b[:, tail], f1[:, tail], ALU.add)
+        for bank, cols in ((b_bank_lo, slice(0, BANK)), (b_bank_mid, slice(BANK, BANK + QUARTER))):
+            nc.vector.tensor_tensor(bb[:, cols], bank[:], f1[:, cols], ALU.add)
 
-        y0 = sb.tile([P, HALF], F32)
-        y1 = sb.tile([P, HALF], F32)
-        g4 = sb.tile([P, HALF], F32)
-        nc.vector.tensor_tensor(y0[:], bb[:].indirect(half("l4", 0)), late[:, 0:HALF], ALU.subtract)
-        nc.sync.dma_start(out[:, 0:HALF], y0[:])
-        nc.scalar.activation(g4[:], bb[:].indirect(half("l4", 1)), ACT.Copy)
-        nc.vector.tensor_tensor(y1[:], g4[:], late[:, HALF:I], ALU.subtract)
-        nc.sync.dma_start(out[:, HALF:I], y1[:])
+        y_lo = sb.tile([P, HALF], F32)
+        y_hi = sb.tile([P, HALF], F32)
+        bb_listed_hi = sb.tile([P, HALF], F32)
+        nc.vector.tensor_tensor(y_lo[:], bb[:].indirect(half_list("idx4", 0)), a_last[:, halves[0]], ALU.subtract)
+        nc.sync.dma_start(out[:, halves[0]], y_lo[:])
+        nc.scalar.activation(bb_listed_hi[:], bb[:].indirect(half_list("idx4", 1)), ACT.Copy)
+        nc.vector.tensor_tensor(y_hi[:], bb_listed_hi[:], a_last[:, halves[1]], ALU.subtract)
+        nc.sync.dma_start(out[:, halves[1]], y_hi[:])

from contextlib import ExitStack

import concourse.mybir as mybir

D, POOL, SLOTS, ROWS = 512, 1024, 512, 128
FLOPS = 2 * D * ROWS * 3 * POOL

F32 = mybir.dt.float32
BF16 = mybir.dt.bfloat16
I32 = mybir.dt.int32
U32 = mybir.dt.uint32
U16 = mybir.dt.uint16
U8 = mybir.dt.uint8
FP8X4 = mybir.dt.float8_e4m3fn_x4
FP4X4 = mybir.dt.float4_e2m1fn_x4
ALU = mybir.AluOpType
ACT = mybir.ActivationFunctionType

P = 128
PACK = 4
BANK = 512
QUARTER = POOL // 4
HALF = SLOTS // 2
HALF_COLS = HALF // 16
CAST_ON_VECTOR = 80


def tile_attend_blendgate_three_kernel(tc, query, keys_words, keys_scales, notes_words, notes_scales,
                                        users_words, users_scales, thr, slope, offs, offs2, offs3, offs4, offs5, out):
    nc = tc.nc
    with ExitStack() as ctx:
        sb = ctx.enter_context(tc.tile_pool(name="sb", bufs=1))
        ps = ctx.enter_context(tc.psum_pool(name="ps", bufs=1))

        planes = {}
        for name in ("notes", "keys", "users"):
            planes[name] = sb.tile([P, POOL], U8, name=name + "_plane", align_bytes=64)
            nc.vector.memset(planes[name][:].bitcast(I32), 0)

        def load_plane(name, scales, quadrants):
            rows = scales[0].bitcast(I32)
            for quad in quadrants:
                nc.sync.dma_start(planes[name][32 * quad:32 * quad + 4, :].bitcast(I32), rows[4 * quad:4 * quad + 4, :])

        lists = {}

        def load_list(name, src):
            lists[name] = sb.tile([P, SLOTS // 16], U16, name=name)
            nc.sync.dma_start(lists[name][:], src)

        def half_list(name, h):
            return lists[name][:, HALF_COLS * h:HALF_COLS * (h + 1)]

        q_raw = sb.tile([P, PACK, ROWS], F32)
        nc.sync.dma_start(q_raw[:], query.rearrange("(p j) q -> p j q", j=PACK))

        notes_lo = sb.tile([P, PACK * BANK], U8, align_bytes=64)
        notes_hi = sb.tile([P, PACK * BANK], U8, align_bytes=64)
        notes_flat = notes_words[0].rearrange("p n t -> p (n t)")
        keys_w = sb.tile([P, 2 * POOL], U8, align_bytes=64)
        users_w = sb.tile([P, 2 * POOL], U8, align_bytes=64)
        thr_t = sb.tile([P, 1], F32)
        slope_t = sb.tile([P, 1], F32)
        f1 = sb.tile([P, POOL], F32)
        nc.gpsimd.dma_start(keys_w[:].bitcast(I32), keys_words[0].bitcast(I32))
        nc.gpsimd.dma_start(users_w[:].bitcast(I32), users_words[0].bitcast(I32))
        nc.gpsimd.dma_start(thr_t[:], thr)
        nc.gpsimd.dma_start(slope_t[:], slope)
        nc.vector.memset(f1[:], 0.0)
        load_plane("notes", notes_scales, range(3))
        nc.sync.dma_start(notes_lo[:].bitcast(I32), notes_flat[:, 0:PACK * BANK].bitcast(I32))
        load_plane("notes", notes_scales, range(3, 4))
        load_list("idx2", offs2)
        nc.sync.dma_start(notes_hi[:].bitcast(I32), notes_flat[:, PACK * BANK:PACK * POOL].bitcast(I32))
        load_plane("keys", keys_scales, range(4))
        load_plane("users", users_scales, range(4))
        load_list("idx", offs)
        load_list("idx3", offs3)
        load_list("idx5", offs5)
        load_list("idx4", offs4)

        q_bf = sb.tile([P, ROWS, PACK], BF16, align_bytes=64)
        warm = sb.tile([P, 1], F32)
        nc.scalar.activation(warm[:], q_raw[:, 0, 0:1], ACT.Sigmoid)
        q_woven = q_raw[:].rearrange("p j q -> p q j")
        nc.vector.tensor_copy(q_bf[:, 0:CAST_ON_VECTOR, :], q_woven[:, 0:CAST_ON_VECTOR, :])
        nc.scalar.copy(q_bf[:, CAST_ON_VECTOR:ROWS, :], q_woven[:, CAST_ON_VECTOR:ROWS, :])
        q_codes = sb.tile([P, ROWS], U32, align_bytes=64)
        q_plane = sb.tile([P, ROWS], U8, align_bytes=64)
        nc.vector.quantize_mx(out=q_codes[:].bitcast(FP8X4), scales=q_plane[:],
                              in_=q_bf[:].rearrange("p q j -> p (q j)"))

        def scores(dst, name, first, width, words, copy):
            bank = ps.tile([P, width], F32, name="%s_bank%d" % (name, first))
            nc.tensor.matmul_mx(out=bank[:], lhsT=q_codes[:].bitcast(FP8X4), lhsT_scale=q_plane[:],
                                rhs=words, rhs_scale=planes[name][:, first:first + width], start=True, stop=True)
            copy(dst[:, first:first + width], bank[:])
            return bank

        on_vector, on_scalar = nc.vector.tensor_copy, nc.scalar.copy

        b = sb.tile([P, POOL], F32)
        b_bank_lo = scores(b, "notes", 0, BANK, notes_lo[:].bitcast(FP8X4), on_scalar)
        b_bank_mid = scores(b, "notes", BANK, QUARTER, notes_hi[:, 0:PACK * QUARTER].bitcast(FP8X4), on_vector)
        scores(b, "notes", BANK + QUARTER, QUARTER, notes_hi[:, PACK * QUARTER:PACK * BANK].bitcast(FP8X4), on_vector)
        b_listed = sb.tile([P, SLOTS], F32)
        nc.scalar.activation(b_listed[:], b[:].indirect(lists["idx2"][:]), ACT.Copy)

        a = sb.tile([P, POOL], F32)
        for first in (0, BANK):
            scores(a, "keys", first, BANK, keys_w[:, 2 * first:2 * (first + BANK)].bitcast(FP4X4), on_vector)
        c0 = sb.tile([P, POOL], F32, tag="c0_then_a_last")
        for first, width, copy in ((0, QUARTER, on_vector), (QUARTER, QUARTER, on_scalar), (BANK, BANK, on_scalar)):
            scores(c0, "users", first, width, users_w[:, 2 * first:2 * (first + width)].bitcast(FP4X4), copy)

        halves = [slice(0, HALF), slice(HALF, SLOTS)]
        r = sb.tile([P, SLOTS], F32)
        for h, cols in enumerate(halves):
            nc.vector.tensor_tensor(r[:, cols], a[:].indirect(half_list("idx", h)), b_listed[:, cols], ALU.subtract)

        s1 = sb.tile([P, SLOTS], F32)
        for h, cols in enumerate(halves):
            nc.scalar.activation(s1[:, cols], c0[:].indirect(half_list("idx3", h)), ACT.Sigmoid,
                                 bias=thr_t[:], scale=slope_t[:])
            nc.vector.tensor_tensor(f1[:].indirect(half_list("idx2", h)), r[:, cols], s1[:, cols], ALU.mult)

        a_last = sb.tile([P, SLOTS], F32, tag="c0_then_a_last")
        nc.scalar.activation(a_last[:], a[:].indirect(lists["idx5"][:]), ACT.Copy)

        bb = sb.tile([P, POOL], F32)
        tail = slice(BANK + QUARTER, POOL)
        nc.gpsimd.tensor_tensor(bb[:, tail], b[:, tail], f1[:, tail], ALU.add)
        for bank, cols in ((b_bank_lo, slice(0, BANK)), (b_bank_mid, slice(BANK, BANK + QUARTER))):
            nc.vector.tensor_tensor(bb[:, cols], bank[:], f1[:, cols], ALU.add)

        y_lo = sb.tile([P, HALF], F32)
        y_hi = sb.tile([P, HALF], F32)
        bb_listed_hi = sb.tile([P, HALF], F32)
        nc.vector.tensor_tensor(y_lo[:], bb[:].indirect(half_list("idx4", 0)), a_last[:, halves[0]], ALU.subtract)
        nc.sync.dma_start(out[:, halves[0]], y_lo[:])
        nc.scalar.activation(bb_listed_hi[:], bb[:].indirect(half_list("idx4", 1)), ACT.Copy)
        nc.vector.tensor_tensor(y_hi[:], bb_listed_hi[:], a_last[:, halves[1]], ALU.subtract)
        nc.sync.dma_start(out[:, halves[1]], y_hi[:])
